import numpy as np
import ml_dtypes


def mxq(x, axis, fmt="e4m3"):
    dtype, down = {"e4m3": (ml_dtypes.float8_e4m3fn, 7), "e5m2": (ml_dtypes.float8_e5m2, 14)}[fmt]
    v = np.moveaxis(np.asarray(x, np.float32).astype(ml_dtypes.bfloat16).astype(np.float64), axis, -1)
    blocks = v.reshape(v.shape[:-1] + (-1, 32))
    amax = np.abs(blocks).max(-1, keepdims=True)
    byte = np.maximum(np.where(amax > 0, np.frexp(amax)[1] - 1 + 127, 0) - down, 1)
    scale = np.exp2(byte - 127.0)
    codes = (blocks / scale).astype(np.float32).astype(dtype).astype(np.float64)
    return np.moveaxis((codes * scale).reshape(v.shape), -1, axis)


WIDE = False


def mx_kscale(k):
    if not WIDE:
        return np.ones(k)
    levels = np.array([10, -10, 5, -5, 0])
    if k % 512:
        return np.exp2(np.random.permutation(np.resize(levels, k // 32))).repeat(32)
    a = np.empty((k // 512, 16))
    for p in range(k // 512):
        a[p, :8] = np.random.permutation(np.resize(levels, 8))
        for g in range(8):
            far = levels[np.abs(levels - a[p, g]) >= 10]
            a[p, g + 8] = far[np.random.randint(len(far))]
    return np.exp2(a.ravel()).repeat(32)


def f64(x):
    return np.asarray(x).astype(np.float64)


def striped(idx):
    return np.tile(idx.reshape(-1, 16).T, (8, 1)).astype(np.uint16)


def unstriped(offs):
    return offs[:16].T.reshape(-1).astype(np.int64)


def pack_weight(w):
    k, n = w.shape
    w = f64(np.asarray(w, np.float32).astype(ml_dtypes.bfloat16)).reshape(k // 32, 32, n)
    amax = np.abs(w).max(1)
    byte = np.clip(np.where(amax > 0, np.frexp(amax)[1] - 1 + 127 - 7, 1), 1, 254)
    scaled = (w * np.exp2(127.0 - byte)[:, None, :]).reshape(k, n).astype(np.float32)
    words = np.ascontiguousarray(scaled.reshape(k // 512, 128, 4, n).transpose(0, 1, 3, 2)).astype(ml_dtypes.float8_e4m3fn).view(np.uint8)
    return words, np.ascontiguousarray(byte.astype(np.uint8).reshape(k // 512, 16, n))


def unpack_weight(words, scales):
    g, p, n, _ = words.shape
    vals = np.ascontiguousarray(words).view(ml_dtypes.float8_e4m3fn).astype(np.float64) * np.repeat(np.exp2(scales.astype(np.float64) - 127.0), 8, axis=1)[..., None]
    return vals.transpose(0, 1, 3, 2).reshape(g * 512, n)


K, T, D, S, V, N = 512, 1024, 8, 512, 64, 512


def setup_inputs():
    n = np.random.standard_normal
    s = mx_kscale(K)[:, None]
    packed = pack_weight(n((K, T)) * s)
    return {
        "x_words": packed[0],
        "x_scales": packed[1],
        "w": (n((K, N)) / np.sqrt(K) / s).astype(np.float32),
        "b": (0.3 * n((N, 1))).astype(np.float32),
        "offs": striped(np.random.permutation(T)[:S]),
    }


def reference(x_words, x_scales, w, b, offs):
    idx = unstriped(offs)
    xq = unpack_weight(x_words, x_scales)[:, idx]
    y = mxq(f64(w), 0, "e4m3").T @ xq
    y = y + f64(b)
    return y.reshape(N, V, D).max(axis=2)

@@ -1,0 +1,103 @@
+from contextlib import ExitStack
+
+import concourse.mybir as mybir
+
+K, T, D, S, V, N = 512, 1024, 8, 512, 64, 512
+FLOPS = 2 * K * N * S
+
+F32 = mybir.dt.float32
+BF16 = mybir.dt.bfloat16
+I32 = mybir.dt.int32
+U32 = mybir.dt.uint32
+U16 = mybir.dt.uint16
+U8 = mybir.dt.uint8
+FP8X4 = mybir.dt.float8_e4m3fn_x4
+
+P = 128
+PACK = 4
+TILES = N // P
+HALF = S // 2
+
+
+def tile_picked_pool_lin_bias_sub_p_kernel(tc, x_words, x_scales, w, b, offs, out):
+    nc = tc.nc
+    with ExitStack() as ctx:
+        keep = ctx.enter_context(tc.tile_pool(name="keep", bufs=1))
+        psum = ctx.enter_context(tc.psum_pool(name="psum", bufs=1))
+
+        offsets = keep.tile([P, S // 16], U16, name="offsets")
+        all_words = keep.tile([P, T], I32, name="all_words", align_bytes=64)
+        all_scales = keep.tile([P, T // 4], I32, name="all_scales", align_bytes=64)
+        got_words = keep.tile([P, S], U32, name="got_words", align_bytes=64)
+        got_scales = keep.tile([P, S], U8, name="got_scales", align_bytes=64)
+        bias = keep.tile([P, TILES], F32, name="bias")
+
+        nc.vector.memset(all_scales[:], 0)
+        nc.sync.dma_start(offsets[:], offs)
+        scale_rows = x_scales[0].bitcast(I32)
+        for q in range(4):
+            nc.scalar.dma_start(all_scales[32 * q : 32 * q + 4, :], scale_rows[4 * q : 4 * q + 4, :])
+
+        w_rows = w.rearrange("(p j) m -> p j m", j=PACK)
+        raw = [keep.tile([P, PACK, P], F32, name="raw%d" % t) for t in range(TILES)]
+        nc.sync.dma_start(raw[0][:], w_rows[:, :, 0:P])
+        nc.sync.dma_start(all_words[:], x_words[0].rearrange("p n t -> p (n t)").bitcast(I32))
+        for t in range(1, TILES):
+            nc.sync.dma_start(raw[t][:], w_rows[:, :, t * P : (t + 1) * P])
+        with nc.allow_non_contiguous_dma(reason="one bias value a partition"):
+            nc.sync.dma_start(bias[:], b.rearrange("(t p) o -> p (t o)", p=P))
+
+        grouped = [keep.tile([P, P, PACK], BF16, name="grouped%d" % t, align_bytes=64) for t in range(TILES)]
+        codes = [keep.tile([P, P], U32, name="codes%d" % t, align_bytes=64) for t in range(TILES)]
+        scales = [keep.tile([P, P], U8, name="scales%d" % t, align_bytes=64) for t in range(TILES)]
+
+        def cast(t):
+            nc.scalar.copy(
+                grouped[t][:].rearrange("p (c i) j -> p c j i", i=4),
+                raw[t][:].rearrange("p j (c i) -> p c j i", i=4),
+            )
+
+        def quantize(t):
+            nc.vector.quantize_mx(
+                out=codes[t][:].bitcast(FP8X4),
+                scales=scales[t][:],
+                in_=grouped[t][:].rearrange("p m j -> p (m j)"),
+            )
+
+        def product(t):
+            pooled = keep.tile([P, V], F32, name="pooled%d" % t)
+            for h in range(2):
+                cols = slice(h * HALF, (h + 1) * HALF)
+                acc = psum.tile([P, HALF], F32, name="acc%d_%d" % (t, h))
+                nc.tensor.matmul_mx(
+                    out=acc[:],
+                    lhsT=codes[t][:].bitcast(FP8X4),
+                    lhsT_scale=scales[t][:],
+                    rhs=got_words[:, cols].bitcast(FP8X4),
+                    rhs_scale=got_scales[:, cols],
+                    start=True,
+                    stop=True,
+                )
+                nc.vector.tensor_reduce(
+                    pooled[:, h * (V // 2) : (h + 1) * (V // 2)],
+                    acc[:].rearrange("p (v d) -> p v d", d=D),
+                    mybir.AxisListType.X,
+                    mybir.AluOpType.max,
+                )
+            result = keep.tile([P, V], F32, name="result%d" % t)
+            nc.scalar.activation(result[:], pooled[:], mybir.ActivationFunctionType.Identity, bias=bias[:, t : t + 1])
+            nc.sync.dma_start(out[t * P : (t + 1) * P, :], result[:])
+
+        for t in range(TILES):
+            cast(t)
+        nc.vector.tensor_copy(got_scales[:], all_scales[:].bitcast(U8).indirect(offsets[:]))
+        quantize(0)
+        for h in range(2):
+            nc.vector.tensor_copy(
+                got_words[:, h * HALF : (h + 1) * HALF],
+                all_words[:].bitcast(U32).indirect(offsets[:, h * (HALF // 16) : (h + 1) * (HALF // 16)]),
+            )
+        for t in range(TILES):
+            if t + 1 < TILES:
+                quantize(t + 1)
+            product(t)

@@ -32,17 +32,15 @@ def tile_picked_pool_lin_bias_sub_p_kernel(tc, x_words, x_scales, w, b, offs, ou
         got_scales = keep.tile([P, S], U8, name="got_scales", align_bytes=64)
         bias = keep.tile([P, TILES], F32, name="bias")
 
-        nc.vector.memset(all_scales[:], 0)
-        nc.sync.dma_start(offsets[:], offs)
         scale_rows = x_scales[0].bitcast(I32)
-        for q in range(4):
-            nc.scalar.dma_start(all_scales[32 * q : 32 * q + 4, :], scale_rows[4 * q : 4 * q + 4, :])
-
         w_rows = w.rearrange("(p j) m -> p j m", j=PACK)
         raw = [keep.tile([P, PACK, P], F32, name="raw%d" % t) for t in range(TILES)]
-        nc.sync.dma_start(raw[0][:], w_rows[:, :, 0:P])
+        nc.vector.memset(all_scales[:], 0)
+        nc.sync.dma_start(offsets[:], offs)
         nc.sync.dma_start(all_words[:], x_words[0].rearrange("p n t -> p (n t)").bitcast(I32))
-        for t in range(1, TILES):
+        for q in range(4):
+            nc.sync.dma_start(all_scales[32 * q : 32 * q + 4, :], scale_rows[4 * q : 4 * q + 4, :])
+        for t in range(TILES):
             nc.sync.dma_start(raw[t][:], w_rows[:, :, t * P : (t + 1) * P])
         with nc.allow_non_contiguous_dma(reason="one bias value a partition"):
             nc.sync.dma_start(bias[:], b.rearrange("(t p) o -> p (t o)", p=P))
@@ -64,40 +62,56 @@ def tile_picked_pool_lin_bias_sub_p_kernel(tc, x_words, x_scales, w, b, offs, ou
                 in_=grouped[t][:].rearrange("p m j -> p (m j)"),
             )
 
-        def product(t):
-            pooled = keep.tile([P, V], F32, name="pooled%d" % t)
-            for h in range(2):
-                cols = slice(h * HALF, (h + 1) * HALF)
-                acc = psum.tile([P, HALF], F32, name="acc%d_%d" % (t, h))
-                nc.tensor.matmul_mx(
-                    out=acc[:],
-                    lhsT=codes[t][:].bitcast(FP8X4),
-                    lhsT_scale=scales[t][:],
-                    rhs=got_words[:, cols].bitcast(FP8X4),
-                    rhs_scale=got_scales[:, cols],
-                    start=True,
-                    stop=True,
-                )
-                nc.vector.tensor_reduce(
-                    pooled[:, h * (V // 2) : (h + 1) * (V // 2)],
-                    acc[:].rearrange("p (v d) -> p v d", d=D),
-                    mybir.AxisListType.X,
-                    mybir.AluOpType.max,
-                )
-            result = keep.tile([P, V], F32, name="result%d" % t)
-            nc.scalar.activation(result[:], pooled[:], mybir.ActivationFunctionType.Identity, bias=bias[:, t : t + 1])
-            nc.sync.dma_start(out[t * P : (t + 1) * P, :], result[:])
+        pooled = [keep.tile([P, V], F32, name="pooled%d" % t) for t in range(TILES)]
+        result = [keep.tile([P, V], F32, name="result%d" % t) for t in range(TILES)]
+
+        def gather_words():
+            nc.vector.tensor_copy(got_words[:], all_words[:].bitcast(U32).indirect(offsets[:]))
+
+        def gather_scales(h):
+            nc.vector.tensor_copy(
+                got_scales[:, h * HALF : (h + 1) * HALF],
+                all_scales[:].bitcast(U8).indirect(offsets[:, h * (HALF // 16) : (h + 1) * (HALF // 16)]),
+            )
+
+        def product(t, h):
+            cols = slice(h * HALF, (h + 1) * HALF)
+            acc = psum.tile([P, HALF], F32, name="acc%d_%d" % (t, h))
+            nc.tensor.matmul_mx(
+                out=acc[:],
+                lhsT=codes[t][:].bitcast(FP8X4),
+                lhsT_scale=scales[t][:],
+                rhs=got_words[:, cols].bitcast(FP8X4),
+                rhs_scale=got_scales[:, cols],
+                start=True,
+                stop=True,
+            )
+            return acc
+
+        def pool(t, h, acc):
+            nc.vector.tensor_reduce(
+                pooled[t][:, h * (V // 2) : (h + 1) * (V // 2)],
+                acc[:].rearrange("p (v d) -> p v d", d=D),
+                mybir.AxisListType.X,
+                mybir.AluOpType.max,
+            )
+
+        def finish(t):
+            nc.scalar.activation(result[t][:], pooled[t][:], mybir.ActivationFunctionType.Identity, bias=bias[:, t : t + 1])
+            nc.sync.dma_start(out[t * P : (t + 1) * P, :], result[t][:])
 
         for t in range(TILES):
             cast(t)
-        nc.vector.tensor_copy(got_scales[:], all_scales[:].bitcast(U8).indirect(offsets[:]))
+        gather_words()
+        gather_scales(0)
         quantize(0)
-        for h in range(2):
-            nc.vector.tensor_copy(
-                got_words[:, h * HALF : (h + 1) * HALF],
-                all_words[:].bitcast(U32).indirect(offsets[:, h * (HALF // 16) : (h + 1) * (HALF // 16)]),
-            )
-        for t in range(TILES):
-            if t + 1 < TILES:
-                quantize(t + 1)
-            product(t)
+        quantize(1)
+        gather_scales(1)
+        for t, h in ((0, 0), (1, 0), (0, 1), (1, 1), (2, 0), (2, 1), (3, 0), (3, 1)):
+            if (t, h) == (1, 0):
+                quantize(2)
+            if (t, h) == (1, 1):
+                quantize(3)
+            pool(t, h, product(t, h))
+            if h == 1:
+                finish(t)

@@ -17,6 +17,8 @@ P = 128
 PACK = 4
 TILES = N // P
 HALF = S // 2
+VH = V // 2
+QUANTIZE_BEFORE = {(0, 0): 1, (0, 1): 2, (1, 1): 3}
 
 
 def tile_picked_pool_lin_bias_sub_p_kernel(tc, x_words, x_scales, w, b, offs, out):
@@ -31,28 +33,33 @@ def tile_picked_pool_lin_bias_sub_p_kernel(tc, x_words, x_scales, w, b, offs, ou
         got_words = keep.tile([P, S], U32, name="got_words", align_bytes=64)
         got_scales = keep.tile([P, S], U8, name="got_scales", align_bytes=64)
         bias = keep.tile([P, TILES], F32, name="bias")
+        raw = [keep.tile([P, PACK, P], F32, name="raw%d" % t, tag="raw%d" % t)[:] for t in range(TILES)]
 
         scale_rows = x_scales[0].bitcast(I32)
         w_rows = w.rearrange("(p j) m -> p j m", j=PACK)
-        raw = [keep.tile([P, PACK, P], F32, name="raw%d" % t) for t in range(TILES)]
         nc.vector.memset(all_scales[:], 0)
         nc.sync.dma_start(offsets[:], offs)
-        nc.sync.dma_start(all_words[:], x_words[0].rearrange("p n t -> p (n t)").bitcast(I32))
+        nc.sync.dma_start(raw[0], w_rows[:, :, 0:P])
         for q in range(4):
-            nc.sync.dma_start(all_scales[32 * q : 32 * q + 4, :], scale_rows[4 * q : 4 * q + 4, :])
-        for t in range(TILES):
-            nc.sync.dma_start(raw[t][:], w_rows[:, :, t * P : (t + 1) * P])
+            queue = nc.sync if q % 2 == 0 else nc.scalar
+            queue.dma_start(all_scales[32 * q : 32 * q + 4, :], scale_rows[4 * q : 4 * q + 4, :])
+        nc.sync.dma_start(all_words[:], x_words[0].rearrange("p n t -> p (n t)").bitcast(I32))
+        for t in range(1, TILES):
+            nc.sync.dma_start(raw[t], w_rows[:, :, t * P : (t + 1) * P])
         with nc.allow_non_contiguous_dma(reason="one bias value a partition"):
             nc.sync.dma_start(bias[:], b.rearrange("(t p) o -> p (t o)", p=P))
 
         grouped = [keep.tile([P, P, PACK], BF16, name="grouped%d" % t, align_bytes=64) for t in range(TILES)]
         codes = [keep.tile([P, P], U32, name="codes%d" % t, align_bytes=64) for t in range(TILES)]
         scales = [keep.tile([P, P], U8, name="scales%d" % t, align_bytes=64) for t in range(TILES)]
+        pooled_last = keep.tile([P, VH], F32, name="pooled_last")
+        biased_last = keep.tile([P, HALF], F32, name="biased_last")
+        result_last = keep.tile([P, V], F32, name="result_last")
 
         def cast(t):
             nc.scalar.copy(
                 grouped[t][:].rearrange("p (c i) j -> p c j i", i=4),
-                raw[t][:].rearrange("p j (c i) -> p c j i", i=4),
+                raw[t].rearrange("p j (c i) -> p c j i", i=4),
             )
 
         def quantize(t):
@@ -62,21 +69,15 @@ def tile_picked_pool_lin_bias_sub_p_kernel(tc, x_words, x_scales, w, b, offs, ou
                 in_=grouped[t][:].rearrange("p m j -> p (m j)"),
             )
 
-        pooled = [keep.tile([P, V], F32, name="pooled%d" % t) for t in range(TILES)]
-        result = [keep.tile([P, V], F32, name="result%d" % t) for t in range(TILES)]
-
-        def gather_words():
-            nc.vector.tensor_copy(got_words[:], all_words[:].bitcast(U32).indirect(offsets[:]))
-
-        def gather_scales(h):
+        def gather_words(h):
             nc.vector.tensor_copy(
-                got_scales[:, h * HALF : (h + 1) * HALF],
-                all_scales[:].bitcast(U8).indirect(offsets[:, h * (HALF // 16) : (h + 1) * (HALF // 16)]),
+                got_words[:, h * HALF : (h + 1) * HALF],
+                all_words[:].bitcast(U32).indirect(offsets[:, h * (HALF // 16) : (h + 1) * (HALF // 16)]),
             )
 
         def product(t, h):
             cols = slice(h * HALF, (h + 1) * HALF)
-            acc = psum.tile([P, HALF], F32, name="acc%d_%d" % (t, h))
+            acc = psum.tile([P, HALF], F32, name="acc%d_%d" % (t, h), tag="acc%d_%d" % (t, h))
             nc.tensor.matmul_mx(
                 out=acc[:],
                 lhsT=codes[t][:].bitcast(FP8X4),
@@ -86,32 +87,49 @@ def tile_picked_pool_lin_bias_sub_p_kernel(tc, x_words, x_scales, w, b, offs, ou
                 start=True,
                 stop=True,
             )
-            return acc
+            return acc[:]
 
-        def pool(t, h, acc):
+        def pool(dst, src):
             nc.vector.tensor_reduce(
-                pooled[t][:, h * (V // 2) : (h + 1) * (V // 2)],
-                acc[:].rearrange("p (v d) -> p v d", d=D),
-                mybir.AxisListType.X,
-                mybir.AluOpType.max,
+                dst, src.rearrange("p (v d) -> p v d", d=D), mybir.AxisListType.X, mybir.AluOpType.max
             )
 
-        def finish(t):
-            nc.scalar.activation(result[t][:], pooled[t][:], mybir.ActivationFunctionType.Identity, bias=bias[:, t : t + 1])
-            nc.sync.dma_start(out[t * P : (t + 1) * P, :], result[t][:])
+        def add_bias(dst, src, t):
+            nc.scalar.activation(dst, src, mybir.ActivationFunctionType.Identity, bias=bias[:, t : t + 1])
 
         for t in range(TILES):
             cast(t)
-        gather_words()
-        gather_scales(0)
+        pooled_a = keep.tile([P, VH], F32, name="pooled_a", tag="raw1")
+        pooled_b = keep.tile([P, V], F32, name="pooled_b", tag="raw2")
+        late = keep.tile([P, 5 * V], F32, name="late", tag="raw3")
+        pooled = [
+            [pooled_a[:], pooled_b[:, 0:VH]],
+            [pooled_b[:, VH:V], late[:, 0:VH]],
+            [late[:, V : V + VH], late[:, V + VH : 2 * V]],
+        ]
+        result = [late[:, (2 + t) * V : (3 + t) * V] for t in range(TILES - 1)]
+
+        nc.vector.tensor_copy(got_scales[:], all_scales[:].bitcast(U8).indirect(offsets[:]))
         quantize(0)
-        quantize(1)
-        gather_scales(1)
-        for t, h in ((0, 0), (1, 0), (0, 1), (1, 1), (2, 0), (2, 1), (3, 0), (3, 1)):
-            if (t, h) == (1, 0):
-                quantize(2)
-            if (t, h) == (1, 1):
-                quantize(3)
-            pool(t, h, product(t, h))
-            if h == 1:
-                finish(t)
+        gather_words(0)
+        gather_words(1)
+        for t in range(TILES - 1):
+            for h in range(2):
+                if (t, h) in QUANTIZE_BEFORE:
+                    quantize(QUANTIZE_BEFORE[t, h])
+                if (t, h) == (TILES - 2, 1):
+                    acc = product(t, h)
+                    add_bias(biased_last[:], product(TILES - 1, 1), TILES - 1)
+                    pool(pooled[t][h], acc)
+                else:
+                    pool(pooled[t][h], product(t, h))
+            if t < 2:
+                for h in range(2):
+                    add_bias(result[t][:, h * VH : (h + 1) * VH], pooled[t][h], t)
+            else:
+                add_bias(result[t], late[:, V : 2 * V], t)
+            nc.sync.dma_start(out[t * P : (t + 1) * P, :], result[t])
+        pool(pooled_last[:], product(TILES - 1, 0))
+        add_bias(result_last[:, 0:VH], pooled_last[:], TILES - 1)
+        pool(result_last[:, VH:V], biased_last[:])
+        nc.sync.dma_start(out[(TILES - 1) * P :, :], result_last[:])

@@ -12,13 +12,15 @@ U32 = mybir.dt.uint32
 U16 = mybir.dt.uint16
 U8 = mybir.dt.uint8
 FP8X4 = mybir.dt.float8_e4m3fn_x4
+MULT = mybir.AluOpType.mult
+ADD = mybir.AluOpType.add
+MAX = mybir.AluOpType.max
 
 P = 128
 PACK = 4
 TILES = N // P
 HALF = S // 2
 VH = V // 2
-QUANTIZE_BEFORE = {(0, 0): 1, (0, 1): 2, (1, 1): 3}
 
 
 def tile_picked_pool_lin_bias_sub_p_kernel(tc, x_words, x_scales, w, b, offs, out):
@@ -27,41 +29,6 @@ def tile_picked_pool_lin_bias_sub_p_kernel(tc, x_words, x_scales, w, b, offs, ou
         keep = ctx.enter_context(tc.tile_pool(name="keep", bufs=1))
         psum = ctx.enter_context(tc.psum_pool(name="psum", bufs=1))
 
-        offsets = keep.tile([P, S // 16], U16, name="offsets")
-        all_words = keep.tile([P, T], I32, name="all_words", align_bytes=64)
-        all_scales = keep.tile([P, T // 4], I32, name="all_scales", align_bytes=64)
-        got_words = keep.tile([P, S], U32, name="got_words", align_bytes=64)
-        got_scales = keep.tile([P, S], U8, name="got_scales", align_bytes=64)
-        bias = keep.tile([P, TILES], F32, name="bias")
-        raw = [keep.tile([P, PACK, P], F32, name="raw%d" % t, tag="raw%d" % t)[:] for t in range(TILES)]
-
-        scale_rows = x_scales[0].bitcast(I32)
-        w_rows = w.rearrange("(p j) m -> p j m", j=PACK)
-        nc.vector.memset(all_scales[:], 0)
-        nc.sync.dma_start(offsets[:], offs)
-        nc.sync.dma_start(raw[0], w_rows[:, :, 0:P])
-        for q in range(4):
-            queue = nc.sync if q % 2 == 0 else nc.scalar
-            queue.dma_start(all_scales[32 * q : 32 * q + 4, :], scale_rows[4 * q : 4 * q + 4, :])
-        nc.sync.dma_start(all_words[:], x_words[0].rearrange("p n t -> p (n t)").bitcast(I32))
-        for t in range(1, TILES):
-            nc.sync.dma_start(raw[t], w_rows[:, :, t * P : (t + 1) * P])
-        with nc.allow_non_contiguous_dma(reason="one bias value a partition"):
-            nc.sync.dma_start(bias[:], b.rearrange("(t p) o -> p (t o)", p=P))
-
-        grouped = [keep.tile([P, P, PACK], BF16, name="grouped%d" % t, align_bytes=64) for t in range(TILES)]
-        codes = [keep.tile([P, P], U32, name="codes%d" % t, align_bytes=64) for t in range(TILES)]
-        scales = [keep.tile([P, P], U8, name="scales%d" % t, align_bytes=64) for t in range(TILES)]
-        pooled_last = keep.tile([P, VH], F32, name="pooled_last")
-        biased_last = keep.tile([P, HALF], F32, name="biased_last")
-        result_last = keep.tile([P, V], F32, name="result_last")
-
-        def cast(t):
-            nc.scalar.copy(
-                grouped[t][:].rearrange("p (c i) j -> p c j i", i=4),
-                raw[t].rearrange("p j (c i) -> p c j i", i=4),
-            )
-
         def quantize(t):
             nc.vector.quantize_mx(
                 out=codes[t][:].bitcast(FP8X4),
@@ -69,67 +36,91 @@ def tile_picked_pool_lin_bias_sub_p_kernel(tc, x_words, x_scales, w, b, offs, ou
                 in_=grouped[t][:].rearrange("p m j -> p (m j)"),
             )
 
-        def gather_words(h):
-            nc.vector.tensor_copy(
-                got_words[:, h * HALF : (h + 1) * HALF],
-                all_words[:].bitcast(U32).indirect(offsets[:, h * (HALF // 16) : (h + 1) * (HALF // 16)]),
-            )
+        def gather_words(lo, hi):
+            nc.vector.tensor_copy(got_words[:, lo:hi], all_words[:].bitcast(U32).indirect(offsets[:, lo // 16 : hi // 16]))
 
-        def product(t, h):
-            cols = slice(h * HALF, (h + 1) * HALF)
-            acc = psum.tile([P, HALF], F32, name="acc%d_%d" % (t, h), tag="acc%d_%d" % (t, h))
+        def gather_scales(lo, hi):
+            nc.vector.tensor_copy(got_scales[:, lo:hi], all_scales[:].bitcast(U8).indirect(offsets[:, lo // 16 : hi // 16]))
+
+        def product(t, lo, hi):
+            acc = psum.tile([P, hi - lo], F32, name="acc%d_%d" % (t, lo), tag="acc%d_%d" % (t, lo))
             nc.tensor.matmul_mx(
                 out=acc[:],
                 lhsT=codes[t][:].bitcast(FP8X4),
                 lhsT_scale=scales[t][:],
-                rhs=got_words[:, cols].bitcast(FP8X4),
-                rhs_scale=got_scales[:, cols],
+                rhs=got_words[:, lo:hi].bitcast(FP8X4),
+                rhs_scale=got_scales[:, lo:hi],
                 start=True,
                 stop=True,
             )
             return acc[:]
 
         def pool(dst, src):
-            nc.vector.tensor_reduce(
-                dst, src.rearrange("p (v d) -> p v d", d=D), mybir.AxisListType.X, mybir.AluOpType.max
-            )
+            nc.vector.tensor_reduce(dst, src.rearrange("p (v d) -> p v d", d=D), mybir.AxisListType.X, MAX)
 
         def add_bias(dst, src, t):
             nc.scalar.activation(dst, src, mybir.ActivationFunctionType.Identity, bias=bias[:, t : t + 1])
 
-        for t in range(TILES):
-            cast(t)
-        pooled_a = keep.tile([P, VH], F32, name="pooled_a", tag="raw1")
-        pooled_b = keep.tile([P, V], F32, name="pooled_b", tag="raw2")
-        late = keep.tile([P, 5 * V], F32, name="late", tag="raw3")
-        pooled = [
-            [pooled_a[:], pooled_b[:, 0:VH]],
-            [pooled_b[:, VH:V], late[:, 0:VH]],
-            [late[:, V : V + VH], late[:, V + VH : 2 * V]],
-        ]
-        result = [late[:, (2 + t) * V : (3 + t) * V] for t in range(TILES - 1)]
-
-        nc.vector.tensor_copy(got_scales[:], all_scales[:].bitcast(U8).indirect(offsets[:]))
+        offsets = keep.tile([P, S // 16], U16, name="offsets")
+        all_words = keep.tile([P, T], I32, name="all_words", align_bytes=64)
+        all_scales = keep.tile([P, T // 4], I32, name="all_scales", align_bytes=64)
+        bias = keep.tile([P, TILES], F32, name="bias")
+        raw0 = keep.tile([P, PACK, 1 * P], F32, name="raw0", tag="raw0", align_bytes=64)
+        raw1 = keep.tile([P, PACK, 1 * P], F32, name="raw1", tag="raw1", align_bytes=64)
+        raw2 = keep.tile([P, PACK, 1 * P], F32, name="raw2", tag="raw2", align_bytes=64)
+        raw3 = keep.tile([P, PACK, 1 * P], F32, name="raw3", tag="raw3", align_bytes=64)
+        scale_rows = x_scales[0].bitcast(I32)
+        w_rows = w.rearrange("(p j) m -> p j m", j=PACK)
+        nc.vector.memset(all_scales[:], 0)
+        nc.sync.dma_start(offsets[:], offs)
+        nc.scalar.dma_start(raw0[:], w_rows[:, :, 0 * P : 1 * P])
+        nc.sync.dma_start(all_scales[0 : 4, :], scale_rows[0 : 4, :])
+        nc.scalar.dma_start(all_scales[32 : 36, :], scale_rows[4 : 8, :])
+        nc.sync.dma_start(all_scales[64 : 68, :], scale_rows[8 : 12, :])
+        nc.scalar.dma_start(all_scales[96 : 100, :], scale_rows[12 : 16, :])
+        nc.sync.dma_start(all_words[:], x_words[0].rearrange("p n t -> p (n t)").bitcast(I32))
+        nc.sync.dma_start(raw1[:], w_rows[:, :, 1 * P : 2 * P])
+        nc.sync.dma_start(raw2[:], w_rows[:, :, 2 * P : 3 * P])
+        nc.sync.dma_start(raw3[:], w_rows[:, :, 3 * P : 4 * P])
+        with nc.allow_non_contiguous_dma(reason="one bias value a partition"):
+            nc.sync.dma_start(bias[:], b.rearrange("(t p) o -> p (t o)", p=P))
+        grouped = [keep.tile([P, P, PACK], BF16, name="grouped%d" % t, tag="grouped%d" % t, align_bytes=64) for t in range(TILES)]
+        codes = [keep.tile([P, P], U32, name="codes%d" % t, align_bytes=64) for t in range(TILES)]
+        scales = [keep.tile([P, P], U8, name="scales%d" % t, align_bytes=64) for t in range(TILES)]
+        nc.scalar.copy(grouped[0][:].rearrange("p (c i) j -> p c j i", i=4), raw0[:, :, 0 * P : 1 * P].rearrange("p j (c i) -> p c j i", i=4))
+        nc.scalar.copy(grouped[1][:].rearrange("p (c i) j -> p c j i", i=4), raw1[:, :, 0 * P : 1 * P].rearrange("p j (c i) -> p c j i", i=4))
+        nc.scalar.copy(grouped[2][:].rearrange("p (c i) j -> p c j i", i=4), raw2[:, :, 0 * P : 1 * P].rearrange("p j (c i) -> p c j i", i=4))
+        nc.scalar.copy(grouped[3][:].rearrange("p (c i) j -> p c j i", i=4), raw3[:, :, 0 * P : 1 * P].rearrange("p j (c i) -> p c j i", i=4))
+        got_words = keep.tile([P, S], U32, name="got_words", align_bytes=64)
+        got_scales = keep.tile([P, S], U8, name="got_scales", align_bytes=64)
+        pooled_a = keep.tile([P, VH], F32, name="pooled_a", tag="raw1", align_bytes=64)
+        pooled_b = keep.tile([P, VH], F32, name="pooled_b", tag="raw2", align_bytes=64)
+        late = keep.tile([P, 5 * V], F32, name="late", tag="raw3", align_bytes=64)
+        pooled_last = keep.tile([P, VH], F32, name="pooled_last")
+        biased_last = keep.tile([P, HALF], F32, name="biased_last")
+        result_last = keep.tile([P, V], F32, name="result_last")
+        gather_scales(0, S)
         quantize(0)
-        gather_words(0)
-        gather_words(1)
-        for t in range(TILES - 1):
-            for h in range(2):
-                if (t, h) in QUANTIZE_BEFORE:
-                    quantize(QUANTIZE_BEFORE[t, h])
-                if (t, h) == (TILES - 2, 1):
-                    acc = product(t, h)
-                    add_bias(biased_last[:], product(TILES - 1, 1), TILES - 1)
-                    pool(pooled[t][h], acc)
-                else:
-                    pool(pooled[t][h], product(t, h))
-            if t < 2:
-                for h in range(2):
-                    add_bias(result[t][:, h * VH : (h + 1) * VH], pooled[t][h], t)
-            else:
-                add_bias(result[t], late[:, V : 2 * V], t)
-            nc.sync.dma_start(out[t * P : (t + 1) * P, :], result[t])
-        pool(pooled_last[:], product(TILES - 1, 0))
-        add_bias(result_last[:, 0:VH], pooled_last[:], TILES - 1)
+        gather_words(0, HALF)
+        gather_words(HALF, S)
+        quantize(1)
+        pool(pooled_a[:], product(0, 0, HALF))
+        quantize(2)
+        pool(pooled_b[:], product(0, HALF, S))
+        add_bias(late[:, 2 * V : 2 * V + VH], pooled_a[:], 0)
+        add_bias(late[:, 2 * V + VH : 3 * V], pooled_b[:], 0)
+        nc.sync.dma_start(out[0:P, :], late[:, 2 * V : 3 * V])
+        quantize(3)
+        pool(late[:, 0:V], product(1, 0, S))
+        add_bias(late[:, 3 * V : 4 * V], late[:, 0:V], 1)
+        nc.sync.dma_start(out[P : 2 * P, :], late[:, 3 * V : 4 * V])
+        acc2 = product(2, 0, S)
+        add_bias(biased_last[:], product(3, HALF, S), 3)
+        acc3 = product(3, 0, HALF)
+        pool(late[:, V : 2 * V], acc2)
+        add_bias(late[:, 4 * V : 5 * V], late[:, V : 2 * V], 2)
+        nc.sync.dma_start(out[2 * P : 3 * P, :], late[:, 4 * V : 5 * V])
+        pool(pooled_last[:], acc3)
+        add_bias(result_last[:, 0:VH], pooled_last[:], 3)
         pool(result_last[:, VH:V], biased_last[:])
-        nc.sync.dma_start(out[(TILES - 1) * P :, :], result_last[:])
+        nc.sync.dma_start(out[3 * P :, :], result_last[:])

@@ -36,24 +36,31 @@ def tile_picked_pool_lin_bias_sub_p_kernel(tc, x_words, x_scales, w, b, offs, ou
                 in_=grouped[t][:].rearrange("p m j -> p (m j)"),
             )
 
+        def words_at(lo, hi):
+            for start, stop, tile in got_words:
+                if start <= lo and hi <= stop:
+                    return tile[:, lo - start : hi - start]
+            raise ValueError("no such slice")
+
         def gather_words(lo, hi):
-            nc.vector.tensor_copy(got_words[:, lo:hi], all_words[:].bitcast(U32).indirect(offsets[:, lo // 16 : hi // 16]))
+            nc.vector.tensor_copy(words_at(lo, hi), all_words[:].bitcast(U32).indirect(offsets[:, lo // 16 : hi // 16]))
 
         def gather_scales(lo, hi):
             nc.vector.tensor_copy(got_scales[:, lo:hi], all_scales[:].bitcast(U8).indirect(offsets[:, lo // 16 : hi // 16]))
 
-        def product(t, lo, hi):
-            acc = psum.tile([P, hi - lo], F32, name="acc%d_%d" % (t, lo), tag="acc%d_%d" % (t, lo))
+        def bank(name, width):
+            return psum.tile([P, width], F32, name=name, tag=name)
+
+        def product(acc, t, lo, hi):
             nc.tensor.matmul_mx(
-                out=acc[:],
+                out=acc,
                 lhsT=codes[t][:].bitcast(FP8X4),
                 lhsT_scale=scales[t][:],
-                rhs=got_words[:, lo:hi].bitcast(FP8X4),
+                rhs=words_at(lo, hi).bitcast(FP8X4),
                 rhs_scale=got_scales[:, lo:hi],
                 start=True,
                 stop=True,
             )
-            return acc[:]
 
         def pool(dst, src):
             nc.vector.tensor_reduce(dst, src.rearrange("p (v d) -> p v d", d=D), mybir.AxisListType.X, MAX)
@@ -61,37 +68,54 @@ def tile_picked_pool_lin_bias_sub_p_kernel(tc, x_words, x_scales, w, b, offs, ou
         def add_bias(dst, src, t):
             nc.scalar.activation(dst, src, mybir.ActivationFunctionType.Identity, bias=bias[:, t : t + 1])
 
+        def cast(t):
+            nc.scalar.copy(grouped[t][:].rearrange("p (c i) j -> p c j i", i=4), raw[t][:].rearrange("p j (c i) -> p c j i", i=4))
+
         offsets = keep.tile([P, S // 16], U16, name="offsets")
         all_words = keep.tile([P, T], I32, name="all_words", align_bytes=64)
         all_scales = keep.tile([P, T // 4], I32, name="all_scales", align_bytes=64)
         bias = keep.tile([P, TILES], F32, name="bias")
-        raw0 = keep.tile([P, PACK, 1 * P], F32, name="raw0", tag="raw0", align_bytes=64)
-        raw1 = keep.tile([P, PACK, 1 * P], F32, name="raw1", tag="raw1", align_bytes=64)
-        raw2 = keep.tile([P, PACK, 1 * P], F32, name="raw2", tag="raw2", align_bytes=64)
-        raw3 = keep.tile([P, PACK, 1 * P], F32, name="raw3", tag="raw3", align_bytes=64)
-        scale_rows = x_scales[0].bitcast(I32)
-        w_rows = w.rearrange("(p j) m -> p j m", j=PACK)
-        nc.vector.memset(all_scales[:], 0)
-        nc.sync.dma_start(offsets[:], offs)
-        nc.scalar.dma_start(raw0[:], w_rows[:, :, 0 * P : 1 * P])
-        nc.sync.dma_start(all_scales[0 : 4, :], scale_rows[0 : 4, :])
-        nc.scalar.dma_start(all_scales[32 : 36, :], scale_rows[4 : 8, :])
-        nc.sync.dma_start(all_scales[64 : 68, :], scale_rows[8 : 12, :])
-        nc.scalar.dma_start(all_scales[96 : 100, :], scale_rows[12 : 16, :])
-        nc.sync.dma_start(all_words[:], x_words[0].rearrange("p n t -> p (n t)").bitcast(I32))
-        nc.sync.dma_start(raw1[:], w_rows[:, :, 1 * P : 2 * P])
-        nc.sync.dma_start(raw2[:], w_rows[:, :, 2 * P : 3 * P])
-        nc.sync.dma_start(raw3[:], w_rows[:, :, 3 * P : 4 * P])
-        with nc.allow_non_contiguous_dma(reason="one bias value a partition"):
-            nc.sync.dma_start(bias[:], b.rearrange("(t p) o -> p (t o)", p=P))
+        raw = [keep.tile([P, PACK, P], F32, name="raw%d" % t, tag="raw%d" % t, align_bytes=64) for t in range(TILES)]
         grouped = [keep.tile([P, P, PACK], BF16, name="grouped%d" % t, tag="grouped%d" % t, align_bytes=64) for t in range(TILES)]
         codes = [keep.tile([P, P], U32, name="codes%d" % t, align_bytes=64) for t in range(TILES)]
         scales = [keep.tile([P, P], U8, name="scales%d" % t, align_bytes=64) for t in range(TILES)]
-        nc.scalar.copy(grouped[0][:].rearrange("p (c i) j -> p c j i", i=4), raw0[:, :, 0 * P : 1 * P].rearrange("p j (c i) -> p c j i", i=4))
-        nc.scalar.copy(grouped[1][:].rearrange("p (c i) j -> p c j i", i=4), raw1[:, :, 0 * P : 1 * P].rearrange("p j (c i) -> p c j i", i=4))
-        nc.scalar.copy(grouped[2][:].rearrange("p (c i) j -> p c j i", i=4), raw2[:, :, 0 * P : 1 * P].rearrange("p j (c i) -> p c j i", i=4))
-        nc.scalar.copy(grouped[3][:].rearrange("p (c i) j -> p c j i", i=4), raw3[:, :, 0 * P : 1 * P].rearrange("p j (c i) -> p c j i", i=4))
-        got_words = keep.tile([P, S], U32, name="got_words", align_bytes=64)
+        scale_rows = x_scales[0].bitcast(I32)
+        w_rows = w.rearrange("(p j) m -> p j m", j=PACK)
+
+        def load_scales(q, queue):
+            queue.dma_start(all_scales[32 * q : 32 * q + 4, :], scale_rows[4 * q : 4 * q + 4, :])
+
+        def load_words(queue):
+            queue.dma_start(all_words[:], x_words[0].rearrange("p n t -> p (n t)").bitcast(I32))
+
+        def load_word_columns(lo, hi, queue):
+            queue.dma_start(all_words[:, lo:hi], x_words[0].rearrange("p n t -> p (n t)").bitcast(I32)[:, lo:hi])
+
+        def load_raw(t, queue):
+            queue.dma_start(raw[t][:], w_rows[:, :, t * P : (t + 1) * P])
+
+        def load_planes(t, lo, hi, queue):
+            queue.dma_start(raw[t][:, lo:hi, :], w_rows[:, lo:hi, t * P : (t + 1) * P])
+
+        def load_bias(queue):
+            with nc.allow_non_contiguous_dma(reason="one bias value a partition"):
+                queue.dma_start(bias[:], b.rearrange("(t p) o -> p (t o)", p=P))
+
+        nc.vector.memset(all_scales[:], 0)
+        nc.sync.dma_start(offsets[:], offs)
+        load_raw(0, nc.scalar)
+        load_scales(0, nc.sync)
+        load_scales(1, nc.scalar)
+        load_scales(2, nc.sync)
+        load_scales(3, nc.scalar)
+        load_words(nc.sync)
+        for t in range(1, TILES):
+            load_raw(t, nc.sync)
+        load_bias(nc.sync)
+        for t in range(TILES):
+            cast(t)
+        picked_words = keep.tile([P, S], U32, name="picked_words", align_bytes=64)
+        got_words = [(0, S, picked_words)]
         got_scales = keep.tile([P, S], U8, name="got_scales", align_bytes=64)
         pooled_a = keep.tile([P, VH], F32, name="pooled_a", tag="raw1", align_bytes=64)
         pooled_b = keep.tile([P, VH], F32, name="pooled_b", tag="raw2", align_bytes=64)
@@ -99,28 +123,41 @@ def tile_picked_pool_lin_bias_sub_p_kernel(tc, x_words, x_scales, w, b, offs, ou
         pooled_last = keep.tile([P, VH], F32, name="pooled_last")
         biased_last = keep.tile([P, HALF], F32, name="biased_last")
         result_last = keep.tile([P, V], F32, name="result_last")
+
         gather_scales(0, S)
         quantize(0)
         gather_words(0, HALF)
-        gather_words(HALF, S)
+        gather_words(HALF, 384)
+        gather_words(384, S)
         quantize(1)
-        pool(pooled_a[:], product(0, 0, HALF))
+        a0 = bank("a0", HALF)
+        b0 = bank("b0", HALF)
+        product(a0[:], 0, 0, HALF)
+        pool(pooled_a[:], a0[:])
         quantize(2)
-        pool(pooled_b[:], product(0, HALF, S))
+        product(b0[:, 0:128], 0, HALF, 384)
+        product(b0[:, 128:256], 0, 384, S)
+        pool(pooled_b[:], b0[:])
         add_bias(late[:, 2 * V : 2 * V + VH], pooled_a[:], 0)
         add_bias(late[:, 2 * V + VH : 3 * V], pooled_b[:], 0)
         nc.sync.dma_start(out[0:P, :], late[:, 2 * V : 3 * V])
         quantize(3)
-        pool(late[:, 0:V], product(1, 0, S))
+        a1 = bank("a1", S)
+        product(a1[:], 1, 0, S)
+        pool(late[:, 0:V], a1[:])
         add_bias(late[:, 3 * V : 4 * V], late[:, 0:V], 1)
         nc.sync.dma_start(out[P : 2 * P, :], late[:, 3 * V : 4 * V])
-        acc2 = product(2, 0, S)
-        add_bias(biased_last[:], product(3, HALF, S), 3)
-        acc3 = product(3, 0, HALF)
-        pool(late[:, V : 2 * V], acc2)
+        a2 = bank("a2", S)
+        product(a2[:], 2, 0, S)
+        b3 = bank("b3", HALF)
+        product(b3[:], 3, HALF, S)
+        add_bias(biased_last[:], b3[:], 3)
+        a3 = bank("a3", HALF)
+        product(a3[:], 3, 0, HALF)
+        pool(late[:, V : 2 * V], a2[:])
         add_bias(late[:, 4 * V : 5 * V], late[:, V : 2 * V], 2)
         nc.sync.dma_start(out[2 * P : 3 * P, :], late[:, 4 * V : 5 * V])
-        pool(pooled_last[:], acc3)
+        pool(pooled_last[:], a3[:])
         add_bias(result_last[:, 0:VH], pooled_last[:], 3)
         pool(result_last[:, VH:V], biased_last[:])
         nc.sync.dma_start(out[3 * P :, :], result_last[:])

@@ -158,6 +158,6 @@ def tile_picked_pool_lin_bias_sub_p_kernel(tc, x_words, x_scales, w, b, offs, ou
         add_bias(late[:, 4 * V : 5 * V], late[:, V : 2 * V], 2)
         nc.sync.dma_start(out[2 * P : 3 * P, :], late[:, 4 * V : 5 * V])
         pool(pooled_last[:], a3[:])
-        add_bias(result_last[:, 0:VH], pooled_last[:], 3)
         pool(result_last[:, VH:V], biased_last[:])
+        nc.vector.tensor_scalar_add(result_last[:, 0:VH], pooled_last[:], bias[:, 3:4])
         nc.sync.dma_start(out[3 * P :, :], result_last[:])

@@ -105,8 +105,8 @@ def tile_picked_pool_lin_bias_sub_p_kernel(tc, x_words, x_scales, w, b, offs, ou
         nc.sync.dma_start(offsets[:], offs)
         load_raw(0, nc.scalar)
         load_scales(0, nc.sync)
-        load_scales(1, nc.scalar)
-        load_scales(2, nc.sync)
+        load_scales(2, nc.scalar)
+        load_scales(1, nc.sync)
         load_scales(3, nc.scalar)
         load_words(nc.sync)
         for t in range(1, TILES):

@@ -66,7 +66,7 @@ def tile_picked_pool_lin_bias_sub_p_kernel(tc, x_words, x_scales, w, b, offs, ou
             nc.vector.tensor_reduce(dst, src.rearrange("p (v d) -> p v d", d=D), mybir.AxisListType.X, MAX)
 
         def add_bias(dst, src, t):
-            nc.scalar.activation(dst, src, mybir.ActivationFunctionType.Identity, bias=bias[:, t : t + 1])
+            nc.scalar.activation(dst, src, mybir.ActivationFunctionType.Identity, bias=bias_blocks[:, t, 0:1])
 
         def cast(t):
             nc.scalar.copy(grouped[t][:].rearrange("p (c i) j -> p c j i", i=4), raw[t][:].rearrange("p j (c i) -> p c j i", i=4))
@@ -74,7 +74,8 @@ def tile_picked_pool_lin_bias_sub_p_kernel(tc, x_words, x_scales, w, b, offs, ou
         offsets = keep.tile([P, S // 16], U16, name="offsets")
         all_words = keep.tile([P, T], I32, name="all_words", align_bytes=64)
         all_scales = keep.tile([P, T // 4], I32, name="all_scales", align_bytes=64)
-        bias = keep.tile([P, TILES], F32, name="bias")
+        bias_blocks = keep.tile([P, TILES, 8], F32, name="bias_blocks")
+        bias = bias_blocks[:, :, 0]
         raw = [keep.tile([P, PACK, P], F32, name="raw%d" % t, tag="raw%d" % t, align_bytes=64) for t in range(TILES)]
         grouped = [keep.tile([P, P, PACK], BF16, name="grouped%d" % t, tag="grouped%d" % t, align_bytes=64) for t in range(TILES)]
         codes = [keep.tile([P, P], U32, name="codes%d" % t, align_bytes=64) for t in range(TILES)]
@@ -99,7 +100,7 @@ def tile_picked_pool_lin_bias_sub_p_kernel(tc, x_words, x_scales, w, b, offs, ou
 
         def load_bias(queue):
             with nc.allow_non_contiguous_dma(reason="one bias value a partition"):
-                queue.dma_start(bias[:], b.rearrange("(t p) o -> p (t o)", p=P))
+                queue.dma_start(bias, b.rearrange("(t p) o -> p (t o)", p=P))
 
         nc.vector.memset(all_scales[:], 0)
         nc.sync.dma_start(offsets[:], offs)
@@ -159,5 +160,5 @@ def tile_picked_pool_lin_bias_sub_p_kernel(tc, x_words, x_scales, w, b, offs, ou
         nc.sync.dma_start(out[2 * P : 3 * P, :], late[:, 4 * V : 5 * V])
         pool(pooled_last[:], a3[:])
         pool(result_last[:, VH:V], biased_last[:])
-        nc.vector.tensor_scalar_add(result_last[:, 0:VH], pooled_last[:], bias[:, 3:4])
+        nc.vector.tensor_scalar_add(result_last[:, 0:VH], pooled_last[:], bias_blocks[:, 3, 0:1])
         nc.sync.dma_start(out[3 * P :, :], result_last[:])

@@ -69,7 +69,7 @@ def tile_picked_pool_lin_bias_sub_p_kernel(tc, x_words, x_scales, w, b, offs, ou
             nc.scalar.activation(dst, src, mybir.ActivationFunctionType.Identity, bias=bias_blocks[:, t, 0:1])
 
         def cast(t):
-            nc.scalar.copy(grouped[t][:].rearrange("p (c i) j -> p c j i", i=4), raw[t][:].rearrange("p j (c i) -> p c j i", i=4))
+            nc.scalar.copy(grouped[t][:].rearrange("p (c i) j -> p c j i", i=2), raw[t][:].rearrange("p j (c i) -> p c j i", i=2))
 
         offsets = keep.tile([P, S // 16], U16, name="offsets")
         all_words = keep.tile([P, T], I32, name="all_words", align_bytes=64)
@@ -89,14 +89,8 @@ def tile_picked_pool_lin_bias_sub_p_kernel(tc, x_words, x_scales, w, b, offs, ou
         def load_words(queue):
             queue.dma_start(all_words[:], x_words[0].rearrange("p n t -> p (n t)").bitcast(I32))
 
-        def load_word_columns(lo, hi, queue):
-            queue.dma_start(all_words[:, lo:hi], x_words[0].rearrange("p n t -> p (n t)").bitcast(I32)[:, lo:hi])
-
         def load_raw(t, queue):
             queue.dma_start(raw[t][:], w_rows[:, :, t * P : (t + 1) * P])
-
-        def load_planes(t, lo, hi, queue):
-            queue.dma_start(raw[t][:, lo:hi, :], w_rows[:, lo:hi, t * P : (t + 1) * P])
 
         def load_bias(queue):
             with nc.allow_non_contiguous_dma(reason="one bias value a partition"):

@@ -98,11 +98,9 @@ def tile_picked_pool_lin_bias_sub_p_kernel(tc, x_words, x_scales, w, b, offs, ou
 
         nc.vector.memset(all_scales[:], 0)
         nc.sync.dma_start(offsets[:], offs)
-        load_raw(0, nc.scalar)
-        load_scales(0, nc.sync)
-        load_scales(2, nc.scalar)
-        load_scales(1, nc.sync)
-        load_scales(3, nc.scalar)
+        load_raw(0, nc.sync)
+        for q in range(4):
+            load_scales(q, nc.sync)
         load_words(nc.sync)
         for t in range(1, TILES):
             load_raw(t, nc.sync)

@@ -84,10 +84,10 @@ def tile_picked_pool_lin_bias_sub_p_kernel(tc, x_words, x_scales, w, b, offs, ou
         w_rows = w.rearrange("(p j) m -> p j m", j=PACK)
 
         def load_scales(q, queue):
-            queue.dma_start(all_scales[32 * q : 32 * q + 4, :], scale_rows[4 * q : 4 * q + 4, :])
+            queue.dma_start(all_scales[q:P:32, :], scale_rows[q:16:4, :])
 
-        def load_words(queue):
-            queue.dma_start(all_words[:], x_words[0].rearrange("p n t -> p (n t)").bitcast(I32))
+        def load_words(lo, hi, queue):
+            queue.dma_start(all_words[:, lo:hi], x_words[0].rearrange("p n t -> p (n t)").bitcast(I32)[:, lo:hi])
 
         def load_raw(t, queue):
             queue.dma_start(raw[t][:], w_rows[:, :, t * P : (t + 1) * P])
@@ -98,10 +98,11 @@ def tile_picked_pool_lin_bias_sub_p_kernel(tc, x_words, x_scales, w, b, offs, ou
 
         nc.vector.memset(all_scales[:], 0)
         nc.sync.dma_start(offsets[:], offs)
+        load_words(0, T // 8, nc.sync)
         load_raw(0, nc.sync)
         for q in range(4):
             load_scales(q, nc.sync)
-        load_words(nc.sync)
+        load_words(T // 8, T, nc.sync)
         for t in range(1, TILES):
             load_raw(t, nc.sync)
         load_bias(nc.sync)

@@ -97,12 +97,12 @@ def tile_picked_pool_lin_bias_sub_p_kernel(tc, x_words, x_scales, w, b, offs, ou
                 queue.dma_start(bias, b.rearrange("(t p) o -> p (t o)", p=P))
 
         nc.vector.memset(all_scales[:], 0)
+        load_words(0, T // 4, nc.sync)
         nc.sync.dma_start(offsets[:], offs)
-        load_words(0, T // 8, nc.sync)
         load_raw(0, nc.sync)
         for q in range(4):
             load_scales(q, nc.sync)
-        load_words(T // 8, T, nc.sync)
+        load_words(T // 4, T, nc.sync)
         for t in range(1, TILES):
             load_raw(t, nc.sync)
         load_bias(nc.sync)

from contextlib import ExitStack

import concourse.mybir as mybir

K, T, D, S, V, N = 512, 1024, 8, 512, 64, 512
FLOPS = 2 * K * N * S

F32 = mybir.dt.float32
BF16 = mybir.dt.bfloat16
I32 = mybir.dt.int32
U32 = mybir.dt.uint32
U16 = mybir.dt.uint16
U8 = mybir.dt.uint8
FP8X4 = mybir.dt.float8_e4m3fn_x4
MULT = mybir.AluOpType.mult
ADD = mybir.AluOpType.add
MAX = mybir.AluOpType.max

P = 128
PACK = 4
TILES = N // P
HALF = S // 2
VH = V // 2


def tile_picked_pool_lin_bias_sub_p_kernel(tc, x_words, x_scales, w, b, offs, out):
    nc = tc.nc
    with ExitStack() as ctx:
        keep = ctx.enter_context(tc.tile_pool(name="keep", bufs=1))
        psum = ctx.enter_context(tc.psum_pool(name="psum", bufs=1))

        def quantize(t):
            nc.vector.quantize_mx(
                out=codes[t][:].bitcast(FP8X4),
                scales=scales[t][:],
                in_=grouped[t][:].rearrange("p m j -> p (m j)"),
            )

        def words_at(lo, hi):
            for start, stop, tile in got_words:
                if start <= lo and hi <= stop:
                    return tile[:, lo - start : hi - start]
            raise ValueError("no such slice")

        def gather_words(lo, hi):
            nc.vector.tensor_copy(words_at(lo, hi), all_words[:].bitcast(U32).indirect(offsets[:, lo // 16 : hi // 16]))

        def gather_scales(lo, hi):
            nc.vector.tensor_copy(got_scales[:, lo:hi], all_scales[:].bitcast(U8).indirect(offsets[:, lo // 16 : hi // 16]))

        def bank(name, width):
            return psum.tile([P, width], F32, name=name, tag=name)

        def product(acc, t, lo, hi):
            nc.tensor.matmul_mx(
                out=acc,
                lhsT=codes[t][:].bitcast(FP8X4),
                lhsT_scale=scales[t][:],
                rhs=words_at(lo, hi).bitcast(FP8X4),
                rhs_scale=got_scales[:, lo:hi],
                start=True,
                stop=True,
            )

        def pool(dst, src):
            nc.vector.tensor_reduce(dst, src.rearrange("p (v d) -> p v d", d=D), mybir.AxisListType.X, MAX)

        def add_bias(dst, src, t):
            nc.scalar.activation(dst, src, mybir.ActivationFunctionType.Identity, bias=bias_blocks[:, t, 0:1])

        def cast(t):
            nc.scalar.copy(grouped[t][:].rearrange("p (c i) j -> p c j i", i=2), raw[t][:].rearrange("p j (c i) -> p c j i", i=2))

        offsets = keep.tile([P, S // 16], U16, name="offsets")
        all_words = keep.tile([P, T], I32, name="all_words", align_bytes=64)
        all_scales = keep.tile([P, T // 4], I32, name="all_scales", align_bytes=64)
        bias_blocks = keep.tile([P, TILES, 8], F32, name="bias_blocks")
        bias = bias_blocks[:, :, 0]
        raw = [keep.tile([P, PACK, P], F32, name="raw%d" % t, tag="raw%d" % t, align_bytes=64) for t in range(TILES)]
        grouped = [keep.tile([P, P, PACK], BF16, name="grouped%d" % t, tag="grouped%d" % t, align_bytes=64) for t in range(TILES)]
        codes = [keep.tile([P, P], U32, name="codes%d" % t, align_bytes=64) for t in range(TILES)]
        scales = [keep.tile([P, P], U8, name="scales%d" % t, align_bytes=64) for t in range(TILES)]
        scale_rows = x_scales[0].bitcast(I32)
        w_rows = w.rearrange("(p j) m -> p j m", j=PACK)

        def load_scales(q, queue):
            queue.dma_start(all_scales[q:P:32, :], scale_rows[q:16:4, :])

        def load_words(lo, hi, queue):
            queue.dma_start(all_words[:, lo:hi], x_words[0].rearrange("p n t -> p (n t)").bitcast(I32)[:, lo:hi])

        def load_raw(t, queue):
            queue.dma_start(raw[t][:], w_rows[:, :, t * P : (t + 1) * P])

        def load_bias(queue):
            with nc.allow_non_contiguous_dma(reason="one bias value a partition"):
                queue.dma_start(bias, b.rearrange("(t p) o -> p (t o)", p=P))

        nc.vector.memset(all_scales[:], 0)
        load_words(0, T // 4, nc.sync)
        nc.sync.dma_start(offsets[:], offs)
        load_raw(0, nc.sync)
        for q in range(4):
            load_scales(q, nc.sync)
        load_words(T // 4, T, nc.sync)
        for t in range(1, TILES):
            load_raw(t, nc.sync)
        load_bias(nc.sync)
        for t in range(TILES):
            cast(t)
        picked_words = keep.tile([P, S], U32, name="picked_words", align_bytes=64)
        got_words = [(0, S, picked_words)]
        got_scales = keep.tile([P, S], U8, name="got_scales", align_bytes=64)
        pooled_a = keep.tile([P, VH], F32, name="pooled_a", tag="raw1", align_bytes=64)
        pooled_b = keep.tile([P, VH], F32, name="pooled_b", tag="raw2", align_bytes=64)
        late = keep.tile([P, 5 * V], F32, name="late", tag="raw3", align_bytes=64)
        pooled_last = keep.tile([P, VH], F32, name="pooled_last")
        biased_last = keep.tile([P, HALF], F32, name="biased_last")
        result_last = keep.tile([P, V], F32, name="result_last")

        gather_scales(0, S)
        quantize(0)
        gather_words(0, HALF)
        gather_words(HALF, 384)
        gather_words(384, S)
        quantize(1)
        a0 = bank("a0", HALF)
        b0 = bank("b0", HALF)
        product(a0[:], 0, 0, HALF)
        pool(pooled_a[:], a0[:])
        quantize(2)
        product(b0[:, 0:128], 0, HALF, 384)
        product(b0[:, 128:256], 0, 384, S)
        pool(pooled_b[:], b0[:])
        add_bias(late[:, 2 * V : 2 * V + VH], pooled_a[:], 0)
        add_bias(late[:, 2 * V + VH : 3 * V], pooled_b[:], 0)
        nc.sync.dma_start(out[0:P, :], late[:, 2 * V : 3 * V])
        quantize(3)
        a1 = bank("a1", S)
        product(a1[:], 1, 0, S)
        pool(late[:, 0:V], a1[:])
        add_bias(late[:, 3 * V : 4 * V], late[:, 0:V], 1)
        nc.sync.dma_start(out[P : 2 * P, :], late[:, 3 * V : 4 * V])
        a2 = bank("a2", S)
        product(a2[:], 2, 0, S)
        b3 = bank("b3", HALF)
        product(b3[:], 3, HALF, S)
        add_bias(biased_last[:], b3[:], 3)
        a3 = bank("a3", HALF)
        product(a3[:], 3, 0, HALF)
        pool(late[:, V : 2 * V], a2[:])
        add_bias(late[:, 4 * V : 5 * V], late[:, V : 2 * V], 2)
        nc.sync.dma_start(out[2 * P : 3 * P, :], late[:, 4 * V : 5 * V])
        pool(pooled_last[:], a3[:])
        pool(result_last[:, VH:V], biased_last[:])
        nc.vector.tensor_scalar_add(result_last[:, 0:VH], pooled_last[:], bias_blocks[:, 3, 0:1])
        nc.sync.dma_start(out[3 * P :, :], result_last[:])
